import numpy as np
import ml_dtypes


def mxq(x, axis, fmt="e4m3"):
    dtype, down = {"e4m3": (ml_dtypes.float8_e4m3fn, 7), "e5m2": (ml_dtypes.float8_e5m2, 14)}[fmt]
    v = np.moveaxis(np.asarray(x, np.float32).astype(ml_dtypes.bfloat16).astype(np.float64), axis, -1)
    blocks = v.reshape(v.shape[:-1] + (-1, 32))
    amax = np.abs(blocks).max(-1, keepdims=True)
    byte = np.maximum(np.where(amax > 0, np.frexp(amax)[1] - 1 + 127, 0) - down, 1)
    scale = np.exp2(byte - 127.0)
    codes = (blocks / scale).astype(np.float32).astype(dtype).astype(np.float64)
    return np.moveaxis((codes * scale).reshape(v.shape), -1, axis)


WIDE = False


def mx_kscale(k):
    if not WIDE:
        return np.ones(k)
    levels = np.array([10, -10, 5, -5, 0])
    if k % 512:
        return np.exp2(np.random.permutation(np.resize(levels, k // 32))).repeat(32)
    a = np.empty((k // 512, 16))
    for p in range(k // 512):
        a[p, :8] = np.random.permutation(np.resize(levels, 8))
        for g in range(8):
            far = levels[np.abs(levels - a[p, g]) >= 10]
            a[p, g + 8] = far[np.random.randint(len(far))]
    return np.exp2(a.ravel()).repeat(32)


def f64(x):
    return np.asarray(x).astype(np.float64)


def striped(idx):
    return np.tile(idx.reshape(-1, 16).T, (8, 1)).astype(np.uint16)


def unstriped(offs):
    return offs[:16].T.reshape(-1).astype(np.int64)


E2M1 = np.array([0.0, 0.5, 1.0, 1.5, 2.0, 3.0, 4.0, 6.0, -0.0, -0.5, -1.0, -1.5, -2.0, -3.0, -4.0, -6.0])


def pack_weight(w, fmt):
    k, n = w.shape
    w = f64(np.asarray(w, np.float32).astype(ml_dtypes.bfloat16)).reshape(k // 32, 32, n)
    amax = np.abs(w).max(1)
    if fmt == "e4m3":
        byte = np.frexp(amax)[1] - 1 + 127 - 7
    else:
        mant, ex = np.frexp(amax / 6.0)
        byte = np.where(mant > 0.5, ex, ex - 1) + 127
    byte = np.clip(np.where(amax > 0, byte, 1), 1, 254)
    scaled = (w * np.exp2(127.0 - byte)[:, None, :]).reshape(k, n).astype(np.float32)
    by_word = np.ascontiguousarray(scaled.reshape(k // 512, 128, 4, n).transpose(0, 1, 3, 2))
    if fmt == "e4m3":
        words = by_word.astype(ml_dtypes.float8_e4m3fn).view(np.uint8)
    else:
        c = by_word.astype(ml_dtypes.float4_e2m1fn).view(np.uint8) & 0xF
        words = (c[..., 0::2] | (c[..., 1::2] << 4)).reshape(k // 512, 128, 2 * n)
    return np.ascontiguousarray(words), np.ascontiguousarray(byte.astype(np.uint8).reshape(k // 512, 16, n))


def unpack_weight(words, scales, fmt):
    g, _, n = scales.shape
    words = np.ascontiguousarray(words).reshape(g, 128, n, -1)
    if fmt == "e4m3":
        vals = words.view(ml_dtypes.float8_e4m3fn).astype(np.float64)
    else:
        nib = np.empty((g, 128, n, 4), np.uint8)
        nib[..., 0::2] = words & 0xF
        nib[..., 1::2] = words >> 4
        vals = E2M1[nib]
    vals = vals * np.repeat(np.exp2(scales.astype(np.float64) - 127.0), 8, axis=1)[..., None]
    return vals.transpose(0, 1, 3, 2).reshape(g * 512, n)


def gelu(v):
    return 0.5 * v * (1.0 + np.tanh(np.sqrt(2.0 / np.pi) * (v + 0.044715 * v**3)))


K, T, S, K2, H, N = 1024, 4096, 1024, 512, 1024, 512

def setup_inputs():
    n = np.random.standard_normal
    s = mx_kscale(K)[:, None]
    s2 = mx_kscale(K2)[:, None]
    u = mx_kscale(H)[:, None]
    d = {}
    d["tab_words"], d["tab_scales"] = pack_weight(n((K, T)) * s, "e4m3")
    d["offs"] = striped(np.random.permutation(T)[:S])
    d["xs_words"], d["xs_scales"] = pack_weight(n((K2, S)) * s2, "e4m3")
    d["w1"] = (n((K, H)) * 2.0 / K**0.5 / s).astype(np.float32)
    d["w2_words"], d["w2_scales"] = pack_weight(n((K2, H)) * 2.0 / K2**0.5 / s2, "e2m1")
    d["gain"] = (np.random.uniform(0.5, 1.5, H) * u[:, 0]).astype(np.float32)
    d["w3"] = (n((H, N)) * 0.6 / H**0.5 / u).astype(np.float32)
    d["wk_words"], d["wk_scales"] = pack_weight(n((K2, N)) / K2**0.5 / s2, "e4m3")
    return d

def reference(tab_words, tab_scales, offs, xs_words, xs_scales, w1, w2_words, w2_scales, gain, w3, wk_words, wk_scales):
    v = unpack_weight(tab_words, tab_scales, "e4m3")[:, unstriped(offs)]
    xs = unpack_weight(xs_words, xs_scales, "e4m3")
    w2 = unpack_weight(w2_words, w2_scales, "e2m1")
    wk = unpack_weight(wk_words, wk_scales, "e4m3")
    a = mxq(f64(w1), 0, "e4m3").T @ v
    b = w2.T @ xs
    h = np.sqrt(a * a + b * b + 1.0) * f64(gain)[:, None]
    hq = mxq(h, 0, "e4m3")
    return mxq(f64(w3), 0, "e4m3").T @ hq + wk.T @ xs

@@ -1,0 +1,280 @@
+from contextlib import ExitStack
+
+import concourse.mybir as mybir
+from concourse.masks import make_identity
+
+K, T, S, K2, H, N = 1024, 4096, 1024, 512, 1024, 512
+FLOPS = 2 * S * (K * H + K2 * H + H * N + K2 * N)
+
+F32 = mybir.dt.float32
+BF16 = mybir.dt.bfloat16
+I32 = mybir.dt.int32
+U32 = mybir.dt.uint32
+U16 = mybir.dt.uint16
+U8 = mybir.dt.uint8
+E4M3X4 = mybir.dt.float8_e4m3fn_x4
+E2M1X4 = mybir.dt.float4_e2m1fn_x4
+ACT = mybir.ActivationFunctionType
+ALU = mybir.AluOpType
+
+P = 128
+PASS = 512
+JT = 128
+JG = 256
+HALF = 512
+
+
+def load_scales(queues, plane, rows):
+    for q, queue in enumerate(queues):
+        queue.dma_start(out=plane[32 * q : 32 * q + 4, :].bitcast(I32), in_=rows[4 * q : 4 * q + 4, :].bitcast(I32))
+
+
+def tile_list_pig_defect_scores_kernel(
+    tc, tab_words, tab_scales, offs, xs_words, xs_scales, w1, w2_words, w2_scales, gain, w3, wk_words, wk_scales, out
+):
+    nc = tc.nc
+    with ExitStack() as ctx:
+        keep = ctx.enter_context(tc.tile_pool(name="keep", bufs=1))
+        ring = ctx.enter_context(tc.tile_pool(name="ring", bufs=2))
+        psum = ctx.enter_context(tc.psum_pool(name="psum", bufs=1))
+
+        def kept(name, shape, dtype):
+            return keep.tile(shape, dtype, name=name, align_bytes=64)
+
+        def staged_in(tag, name, shape, dtype):
+            return keep.tile(shape, dtype, name=name, tag=tag, align_bytes=64)
+
+        xs_s = kept("xs_s", [P, S], U8)
+        w2_s_raw = staged_in("stage_b", "w2_s_raw", [P, H], U8)
+        tab_s = staged_in("planes", "tab_s", [P, T], U8)
+        gain_rows = kept("gain_rows", [P, 2 * P], F32)
+        warm = kept("warm", [P, 2], F32)
+        nc.gpsimd.memset(xs_s[:].bitcast(I32), 0)
+        nc.gpsimd.memset(w2_s_raw[:].bitcast(I32), 0)
+        nc.gpsimd.memset(warm[:, 0:1], 1.0)
+        nc.vector.memset(tab_s[:].bitcast(I32), 0)
+        nc.vector.memset(gain_rows[:], 0.0)
+
+        xs_w = kept("xs_w", [P, S], I32)
+        nc.sync.dma_start(out=xs_w[:], in_=xs_words[0].rearrange("p c i -> p (c i)").bitcast(I32))
+        w2_w_raw = staged_in("stage_a", "w2_w_raw", [P, H // 2], I32)
+        nc.sync.dma_start(out=w2_w_raw[:], in_=w2_words[0].bitcast(I32))
+        offsets = keep.tile([P, S // 16], U16, name="offsets")
+        nc.sync.dma_start(offsets[:], offs)
+        tab_w = {}
+
+        def load_table(a, tag):
+            tab_w[a] = staged_in(tag, "tab_w%d" % a, [P, T], I32)
+            nc.sync.dma_start(out=tab_w[a][:], in_=tab_words[a].rearrange("p t i -> p (t i)").bitcast(I32))
+
+        load_table(0, "stage_c")
+        load_scales([nc.scalar] * 4, xs_s, xs_scales[0])
+        load_scales([nc.scalar] * 2 + [nc.gpsimd] * 2, w2_s_raw, w2_scales[0])
+        nc.scalar.activation(out=warm[:, 1:2], in_=warm[:, 0:1], func=ACT.Sqrt)
+        for q in range(4):
+            nc.gpsimd.dma_start(
+                out=tab_s[32 * q : 32 * q + 8, :].bitcast(I32), in_=tab_scales[:, 4 * q : 4 * q + 4, :].bitcast(I32)
+            )
+
+        nc.gpsimd.dma_start(
+            out=gain_rows[0:4, :].rearrange("t (b i) -> t b i", i=8), in_=gain.rearrange("(b t i) -> t b i", t=4, i=8)
+        )
+
+        w2_w = kept("w2_w", [P, H // 2], I32)
+        w2_s = kept("w2_s", [P, H], U8)
+        nc.vector.tensor_copy(
+            out=w2_w[:].rearrange("p (c t g e) -> p c t g e", c=2, t=4, e=4),
+            in_=w2_w_raw[:].rearrange("p (c g t e) -> p c t g e", c=2, t=4, e=4),
+        )
+        nc.vector.tensor_copy(
+            out=w2_s[:].bitcast(I32).rearrange("p (c t g e) -> p c t g e", c=2, t=4, e=2),
+            in_=w2_s_raw[:].bitcast(I32).rearrange("p (c g t e) -> p c t g e", c=2, t=4, e=2),
+        )
+
+        w1_raw = {}
+
+        def load_w1(c):
+            both = staged_in("stage_a", "w1_raw%d" % c, [P, 2 * 4 * PASS], F32)
+            for a in range(2):
+                w1_raw[c, a] = both[:, 4 * PASS * a : 4 * PASS * (a + 1)].rearrange("p (j n) -> p j n", j=4)
+                rows = w1[PASS * a : PASS * (a + 1), PASS * c : PASS * (c + 1)]
+                nc.sync.dma_start(out=w1_raw[c, a], in_=rows.rearrange("(p j) n -> p j n", j=4))
+
+        load_w1(0)
+        load_table(1, "stage_b")
+
+        ident = kept("ident", [P, P], F32)
+        make_identity(nc, ident[:])
+        gain_ps = psum.tile([P, 2, P], F32, name="gain_ps")
+        for c in range(2):
+            nc.tensor.transpose(gain_ps[:, c, :], gain_rows[:, P * c : P * (c + 1)], ident[:])
+
+        order = [(0, 0), (0, 1), (0, 2), (1, 0), (0, 3), (1, 1), (1, 2), (1, 3)]
+
+        b_sq = {}
+        for c, g in order:
+            b_sq[c, g] = kept("b_sq%d%d" % (c, g), [P, JG, 4], F32)
+            for u in range(2):
+                j0 = JG * g + JT * u
+                bank = psum.tile([P, 4, JT], F32, name="ab_bank", bufs=3)
+                for t in range(4):
+                    r0 = PASS * c + P * t
+                    nc.tensor.matmul_mx(
+                        out=bank[:, t, :],
+                        lhsT=w2_w[:, r0 // 2 : (r0 + P) // 2].bitcast(E2M1X4),
+                        lhsT_scale=w2_s[:, r0 : r0 + P],
+                        rhs=xs_w[:, j0 : j0 + JT].bitcast(E4M3X4),
+                        rhs_scale=xs_s[:, j0 : j0 + JT],
+                        start=True,
+                        stop=True,
+                    )
+                nc.scalar.activation(
+                    out=b_sq[c, g][:, JT * u : JT * (u + 1), :], in_=bank[:].rearrange("p t n -> p n t"), func=ACT.Square
+                )
+
+        v_w = {}
+        v_s = {}
+
+        def gather_words(a, h):
+            v_w[a, h] = kept("v_w%d%d" % (a, h), [P, HALF], U32)
+            nc.vector.tensor_copy(v_w[a, h][:], tab_w[a][:].bitcast(U32).indirect(offsets[:, 32 * h : 32 * (h + 1)]))
+
+        def gather_scales(h):
+            v_s[h] = kept("v_s%d" % h, [P, HALF], U8)
+            nc.vector.tensor_copy(v_s[h][:], tab_s[:].indirect(offsets[:, 32 * h : 32 * (h + 1)]))
+
+        w1_q = {}
+        w1_s = {}
+        w1_bf = {}
+
+        def round_w1(c, a):
+            for t in range(4):
+                w1_bf[c, a, t] = ring.tile([P, P, 4], BF16, name="w1_bf", bufs=8, align_bytes=64)
+                src = w1_raw[c, a].rearrange("p j (g t e i) -> p t g e j i", t=4, e=2, i=4)[:, t]
+                dst = w1_bf[c, a, t][:].rearrange("p (g e i) j -> p g e j i", e=2, i=4)
+                nc.vector.tensor_copy(out=dst, in_=src)
+
+        def quantise_w1(c, a):
+            for t in range(4):
+                w1_q[c, a, t] = kept("w1_q%d%d%d" % (c, a, t), [P, P], U32)
+                w1_s[c, a, t] = kept("w1_s%d%d%d" % (c, a, t), [P, P], U8)
+                nc.vector.quantize_mx(
+                    out=w1_q[c, a, t][:].bitcast(E4M3X4),
+                    scales=w1_s[c, a, t][:],
+                    in_=w1_bf[c, a, t][:].rearrange("p m j -> p (m j)"),
+                )
+
+        gather_words(0, 0)
+        gather_words(0, 1)
+        round_w1(0, 0)
+        quantise_w1(0, 0)
+        gather_scales(0)
+        gather_scales(1)
+        round_w1(0, 1)
+        quantise_w1(0, 1)
+        gather_words(1, 0)
+        gather_words(1, 1)
+
+        wk_w = staged_in("stage_c", "wk_w", [P, N], I32)
+        nc.sync.dma_start(out=wk_w[:], in_=wk_words[0].rearrange("p c i -> p (c i)").bitcast(I32))
+        wk_s = staged_in("planes", "wk_s", [P, N], U8)
+        nc.gpsimd.memset(wk_s[:].bitcast(I32), 0)
+        load_scales([nc.sync] * 4, wk_s, wk_scales[0])
+        load_w1(1)
+        w3_both = staged_in("stage_b", "w3_raw", [P, 2 * 4 * N], F32)
+        w3_raw = {}
+        for c in range(2):
+            w3_raw[c] = w3_both[:, 4 * N * c : 4 * N * (c + 1)].rearrange("p (t n) -> p t n", t=4)
+            rows = w3[PASS * c : PASS * (c + 1), :].rearrange("(g t i) n -> t g i n", t=4, i=8)
+            for t in range(4):
+                nc.sync.dma_start(out=w3_raw[c][:, t, :], in_=rows[t])
+
+        w3_q = {}
+        w3_s = {}
+
+        def quantise_w3(c, engine_copy):
+            w3_bf = ring.tile([P, N, 4], BF16, name="w3_bf", align_bytes=64)
+            engine_copy(
+                out=w3_bf[:].rearrange("p (m i) t -> p m t i", i=4), in_=w3_raw[c].rearrange("p t (m i) -> p m t i", i=4)
+            )
+            w3_q[c] = kept("w3_q%d" % c, [P, N], U32)
+            w3_s[c] = kept("w3_s%d" % c, [P, N], U8)
+            nc.vector.quantize_mx(
+                out=w3_q[c][:].bitcast(E4M3X4), scales=w3_s[c][:], in_=w3_bf[:].rearrange("p m t -> p (m t)")
+            )
+
+        h_q = {}
+        h_s = {}
+
+        def make_h(c, g):
+            a_sq = ring.tile([P, JG, 4], F32, name="a_sq")
+            for u in range(2):
+                j0 = JG * g + JT * u
+                h, jj = divmod(j0, HALF)
+                bank = psum.tile([P, 4, JT], F32, name="ab_bank", bufs=3)
+                for t in range(4):
+                    for a in range(2):
+                        nc.tensor.matmul_mx(
+                            out=bank[:, t, :],
+                            lhsT=w1_q[c, a, t][:].bitcast(E4M3X4),
+                            lhsT_scale=w1_s[c, a, t][:],
+                            rhs=v_w[a, h][:, jj : jj + JT].bitcast(E4M3X4),
+                            rhs_scale=v_s[h][4 * a :, jj : jj + JT],
+                            start=(a == 0),
+                            stop=(a == 1),
+                        )
+                nc.scalar.activation(
+                    out=a_sq[:, JT * u : JT * (u + 1), :], in_=bank[:].rearrange("p t n -> p n t"), func=ACT.Square
+                )
+            total = ring.tile([P, JG, 4], F32, name="total")
+            nc.vector.tensor_tensor(out=total[:], in0=a_sq[:], in1=b_sq[c, g][:], op=ALU.add)
+            root = ring.tile([P, JG, 4], F32, name="root")
+            nc.scalar.activation(out=root[:], in_=total[:], func=ACT.Sqrt, bias=1.0)
+            h_bf = ring.tile([P, JG, 4], BF16, name="h_bf", align_bytes=64)
+            nc.vector.tensor_tensor(
+                out=h_bf[:], in0=root[:], in1=gain_ps[:, c, 0:4].unsqueeze(1).broadcast_to([P, JG, 4]), op=ALU.mult
+            )
+            h_q[c, g] = kept("h_q%d%d" % (c, g), [P, JG], U32)
+            h_s[c, g] = kept("h_s%d%d" % (c, g), [P, JG], U8)
+            nc.vector.quantize_mx(
+                out=h_q[c, g][:].bitcast(E4M3X4), scales=h_s[c, g][:], in_=h_bf[:].rearrange("p n t -> p (n t)")
+            )
+
+        out_view = out.rearrange("(m p) j -> p m j", p=P)
+
+        def make_out(g):
+            cols = slice(JG * g, JG * (g + 1))
+            for pair in range(2):
+                bank = psum.tile([P, 2, JG], F32, name="out_bank", bufs=4)
+                passes = [(wk_w, wk_s, xs_w[:, cols], xs_s[:, cols])]
+                passes.extend((w3_q[c], w3_s[c], h_q[c, g][:], h_s[c, g][:]) for c in range(2))
+                for step, (w_codes, w_scales, x_codes, x_scales) in enumerate(passes):
+                    for m in range(2):
+                        n0 = P * (2 * pair + m)
+                        nc.tensor.matmul_mx(
+                            out=bank[:, m, :],
+                            lhsT=w_codes[:, n0 : n0 + P].bitcast(E4M3X4),
+                            lhsT_scale=w_scales[:, n0 : n0 + P],
+                            rhs=x_codes.bitcast(E4M3X4),
+                            rhs_scale=x_scales,
+                            start=(step == 0 and m == 0),
+                            stop=(step == 2 and m == 1),
+                        )
+                staged = ring.tile([P, 2, JG], F32, name="staged", bufs=4)
+                nc.scalar.copy(out=staged[:], in_=bank[:])
+                nc.sync.dma_start(out=out_view[:, 2 * pair : 2 * pair + 2, cols], in_=staged[:])
+
+        for step, (c, g) in enumerate(order):
+            make_h(c, g)
+            if step == 0:
+                round_w1(1, 0)
+                quantise_w1(1, 0)
+            if step == 1:
+                round_w1(1, 1)
+                quantise_w1(1, 1)
+            if step == 2:
+                quantise_w3(0, nc.scalar.copy)
+            if step == 3:
+                quantise_w3(1, nc.vector.tensor_copy)
+            if c == 1:
+                make_out(g)

@@ -24,8 +24,8 @@ JG = 256
 HALF = 512
 
 
-def load_scales(queues, plane, rows):
-    for q, queue in enumerate(queues):
+def load_scales(queue, plane, rows):
+    for q in range(4):
         queue.dma_start(out=plane[32 * q : 32 * q + 4, :].bitcast(I32), in_=rows[4 * q : 4 * q + 4, :].bitcast(I32))
 
 
@@ -41,44 +41,63 @@ def tile_list_pig_defect_scores_kernel(
         def kept(name, shape, dtype):
             return keep.tile(shape, dtype, name=name, align_bytes=64)
 
-        def staged_in(tag, name, shape, dtype):
-            return keep.tile(shape, dtype, name=name, tag=tag, align_bytes=64)
-
         xs_s = kept("xs_s", [P, S], U8)
-        w2_s_raw = staged_in("stage_b", "w2_s_raw", [P, H], U8)
-        tab_s = staged_in("planes", "tab_s", [P, T], U8)
+        w2_s_raw = kept("w2_s_raw", [P, H], U8)
+        tab_s = kept("tab_s", [P, T], U8)
+        wk_s = kept("wk_s", [P, N], U8)
         gain_rows = kept("gain_rows", [P, 2 * P], F32)
         warm = kept("warm", [P, 2], F32)
-        nc.gpsimd.memset(xs_s[:].bitcast(I32), 0)
         nc.gpsimd.memset(w2_s_raw[:].bitcast(I32), 0)
-        nc.gpsimd.memset(warm[:, 0:1], 1.0)
+        nc.gpsimd.memset(xs_s[:].bitcast(I32), 0)
         nc.vector.memset(tab_s[:].bitcast(I32), 0)
+        nc.vector.memset(warm[:, 0:1], 1.0)
         nc.vector.memset(gain_rows[:], 0.0)
+        nc.vector.memset(wk_s[:].bitcast(I32), 0)
+        nc.scalar.activation(out=warm[:, 1:2], in_=warm[:, 0:1], func=ACT.Sqrt)
 
-        xs_w = kept("xs_w", [P, S], I32)
-        nc.sync.dma_start(out=xs_w[:], in_=xs_words[0].rearrange("p c i -> p (c i)").bitcast(I32))
-        w2_w_raw = staged_in("stage_a", "w2_w_raw", [P, H // 2], I32)
-        nc.sync.dma_start(out=w2_w_raw[:], in_=w2_words[0].bitcast(I32))
         offsets = keep.tile([P, S // 16], U16, name="offsets")
         nc.sync.dma_start(offsets[:], offs)
-        tab_w = {}
-
-        def load_table(a, tag):
-            tab_w[a] = staged_in(tag, "tab_w%d" % a, [P, T], I32)
-            nc.sync.dma_start(out=tab_w[a][:], in_=tab_words[a].rearrange("p t i -> p (t i)").bitcast(I32))
-
-        load_table(0, "stage_c")
-        load_scales([nc.scalar] * 4, xs_s, xs_scales[0])
-        load_scales([nc.scalar] * 2 + [nc.gpsimd] * 2, w2_s_raw, w2_scales[0])
-        nc.scalar.activation(out=warm[:, 1:2], in_=warm[:, 0:1], func=ACT.Sqrt)
+        xs_w = kept("xs_w", [P, S], I32)
+        nc.sync.dma_start(out=xs_w[:], in_=xs_words[0].rearrange("p c i -> p (c i)").bitcast(I32))
+        w2_w_raw = kept("w2_w_raw", [P, H // 2], I32)
+        nc.sync.dma_start(out=w2_w_raw[:], in_=w2_words[0].bitcast(I32))
+        load_scales(nc.sync, w2_s_raw, w2_scales[0])
         for q in range(4):
             nc.gpsimd.dma_start(
                 out=tab_s[32 * q : 32 * q + 8, :].bitcast(I32), in_=tab_scales[:, 4 * q : 4 * q + 4, :].bitcast(I32)
             )
+        tab_w = [kept("tab_w%d" % a, [P, T], I32) for a in range(2)]
 
+        def load_table(a):
+            nc.sync.dma_start(out=tab_w[a][:], in_=tab_words[a].rearrange("p t i -> p (t i)").bitcast(I32))
+
+        w1_raw = {}
+
+        def load_w1(c, a, lo, hi):
+            w1_raw[c, a, lo] = kept("w1_raw%d%d%d" % (c, a, lo), [P, 4, 32 * (hi - lo)], F32)
+            rows = w1[PASS * a : PASS * (a + 1), PASS * c + 32 * lo : PASS * c + 32 * hi]
+            nc.sync.dma_start(out=w1_raw[c, a, lo][:], in_=rows.rearrange("(p j) n -> p j n", j=4))
+
+        load_table(0)
+        load_scales(nc.sync, xs_s, xs_scales[0])
+        load_w1(0, 0, 0, 16)
+        load_table(1)
+        load_w1(0, 1, 0, 8)
+        load_w1(0, 1, 8, 16)
+        load_w1(1, 0, 0, 16)
+        load_w1(1, 1, 0, 16)
         nc.gpsimd.dma_start(
             out=gain_rows[0:4, :].rearrange("t (b i) -> t b i", i=8), in_=gain.rearrange("(b t i) -> t b i", t=4, i=8)
         )
+        load_scales(nc.gpsimd, wk_s, wk_scales[0])
+        wk_w = kept("wk_w", [P, N], I32)
+        nc.sync.dma_start(out=wk_w[:], in_=wk_words[0].rearrange("p c i -> p (c i)").bitcast(I32))
+        w3_raw = {}
+        for c in range(2):
+            w3_raw[c] = kept("w3_raw%d" % c, [P, 4, N], F32)
+            rows = w3[PASS * c : PASS * (c + 1), :].rearrange("(g t i) n -> t g i n", t=4, i=8)
+            for t in range(4):
+                nc.sync.dma_start(out=w3_raw[c][:, t, :], in_=rows[t])
 
         w2_w = kept("w2_w", [P, H // 2], I32)
         w2_s = kept("w2_s", [P, H], U8)
@@ -91,25 +110,13 @@ def tile_list_pig_defect_scores_kernel(
             in_=w2_s_raw[:].bitcast(I32).rearrange("p (c g t e) -> p c t g e", c=2, t=4, e=2),
         )
 
-        w1_raw = {}
-
-        def load_w1(c):
-            both = staged_in("stage_a", "w1_raw%d" % c, [P, 2 * 4 * PASS], F32)
-            for a in range(2):
-                w1_raw[c, a] = both[:, 4 * PASS * a : 4 * PASS * (a + 1)].rearrange("p (j n) -> p j n", j=4)
-                rows = w1[PASS * a : PASS * (a + 1), PASS * c : PASS * (c + 1)]
-                nc.sync.dma_start(out=w1_raw[c, a], in_=rows.rearrange("(p j) n -> p j n", j=4))
-
-        load_w1(0)
-        load_table(1, "stage_b")
-
         ident = kept("ident", [P, P], F32)
         make_identity(nc, ident[:])
         gain_ps = psum.tile([P, 2, P], F32, name="gain_ps")
         for c in range(2):
             nc.tensor.transpose(gain_ps[:, c, :], gain_rows[:, P * c : P * (c + 1)], ident[:])
 
-        order = [(0, 0), (0, 1), (0, 2), (1, 0), (0, 3), (1, 1), (1, 2), (1, 3)]
+        order = [(c, g) for c in range(2) for g in range(4)]
 
         b_sq = {}
         for c, g in order:
@@ -147,55 +154,51 @@ def tile_list_pig_defect_scores_kernel(
         w1_s = {}
         w1_bf = {}
 
-        def round_w1(c, a):
-            for t in range(4):
-                w1_bf[c, a, t] = ring.tile([P, P, 4], BF16, name="w1_bf", bufs=8, align_bytes=64)
-                src = w1_raw[c, a].rearrange("p j (g t e i) -> p t g e j i", t=4, e=2, i=4)[:, t]
-                dst = w1_bf[c, a, t][:].rearrange("p (g e i) j -> p g e j i", e=2, i=4)
-                nc.vector.tensor_copy(out=dst, in_=src)
+        def rounded_tile(name, columns):
+            return ring.tile([P, columns, 4], BF16, name=name, tag="rounded", align_bytes=64)
 
-        def quantise_w1(c, a):
+        def round_w1(c, a, lo, hi, engine_copy):
+            if lo == 0:
+                w1_bf[c, a] = rounded_tile("w1_bf", PASS)
             for t in range(4):
-                w1_q[c, a, t] = kept("w1_q%d%d%d" % (c, a, t), [P, P], U32)
-                w1_s[c, a, t] = kept("w1_s%d%d%d" % (c, a, t), [P, P], U8)
+                src = w1_raw[c, a, lo][:].rearrange("p j (g t e i) -> p t g e j i", t=4, e=2, i=4)[:, t]
+                dst = w1_bf[c, a][:, P * t + 8 * lo : P * t + 8 * hi, :].rearrange("p (g e i) j -> p g e j i", e=2, i=4)
+                engine_copy(out=dst, in_=src)
+
+        def quantise_w1(c, a, pieces):
+            width = PASS // pieces
+            for piece in range(pieces):
+                codes = kept("w1_q%d%d%d" % (c, a, piece), [P, width], U32)
+                scales = kept("w1_s%d%d%d" % (c, a, piece), [P, width], U8)
                 nc.vector.quantize_mx(
-                    out=w1_q[c, a, t][:].bitcast(E4M3X4),
-                    scales=w1_s[c, a, t][:],
-                    in_=w1_bf[c, a, t][:].rearrange("p m j -> p (m j)"),
+                    out=codes[:].bitcast(E4M3X4),
+                    scales=scales[:],
+                    in_=w1_bf[c, a][:, width * piece : width * (piece + 1), :].rearrange("p m j -> p (m j)"),
                 )
+                for m0 in range(0, width, P):
+                    t = (width * piece + m0) // P
+                    w1_q[c, a, t] = codes[:, m0 : m0 + P]
+                    w1_s[c, a, t] = scales[:, m0 : m0 + P]
 
-        gather_words(0, 0)
-        gather_words(0, 1)
-        round_w1(0, 0)
-        quantise_w1(0, 0)
         gather_scales(0)
         gather_scales(1)
-        round_w1(0, 1)
-        quantise_w1(0, 1)
+        gather_words(0, 0)
+        gather_words(0, 1)
+        round_w1(0, 0, 0, 16, nc.vector.tensor_copy)
+        quantise_w1(0, 0, 1)
         gather_words(1, 0)
         gather_words(1, 1)
-
-        wk_w = staged_in("stage_c", "wk_w", [P, N], I32)
-        nc.sync.dma_start(out=wk_w[:], in_=wk_words[0].rearrange("p c i -> p (c i)").bitcast(I32))
-        wk_s = staged_in("planes", "wk_s", [P, N], U8)
-        nc.gpsimd.memset(wk_s[:].bitcast(I32), 0)
-        load_scales([nc.sync] * 4, wk_s, wk_scales[0])
-        load_w1(1)
-        w3_both = staged_in("stage_b", "w3_raw", [P, 2 * 4 * N], F32)
-        w3_raw = {}
-        for c in range(2):
-            w3_raw[c] = w3_both[:, 4 * N * c : 4 * N * (c + 1)].rearrange("p (t n) -> p t n", t=4)
-            rows = w3[PASS * c : PASS * (c + 1), :].rearrange("(g t i) n -> t g i n", t=4, i=8)
-            for t in range(4):
-                nc.sync.dma_start(out=w3_raw[c][:, t, :], in_=rows[t])
+        round_w1(0, 1, 0, 8, nc.vector.tensor_copy)
+        round_w1(0, 1, 8, 16, nc.vector.tensor_copy)
+        quantise_w1(0, 1, 4)
 
         w3_q = {}
         w3_s = {}
 
         def quantise_w3(c, engine_copy):
-            w3_bf = ring.tile([P, N, 4], BF16, name="w3_bf", align_bytes=64)
+            w3_bf = rounded_tile("w3_bf", N)
             engine_copy(
-                out=w3_bf[:].rearrange("p (m i) t -> p m t i", i=4), in_=w3_raw[c].rearrange("p t (m i) -> p m t i", i=4)
+                out=w3_bf[:].rearrange("p (m i) t -> p m t i", i=4), in_=w3_raw[c][:].rearrange("p t (m i) -> p m t i", i=4)
             )
             w3_q[c] = kept("w3_q%d" % c, [P, N], U32)
             w3_s[c] = kept("w3_s%d" % c, [P, N], U8)
@@ -207,7 +210,7 @@ def tile_list_pig_defect_scores_kernel(
         h_s = {}
 
         def make_h(c, g):
-            a_sq = ring.tile([P, JG, 4], F32, name="a_sq")
+            a_sq = ring.tile([P, JG, 4], F32, name="a_sq", bufs=4)
             for u in range(2):
                 j0 = JG * g + JT * u
                 h, jj = divmod(j0, HALF)
@@ -216,8 +219,8 @@ def tile_list_pig_defect_scores_kernel(
                     for a in range(2):
                         nc.tensor.matmul_mx(
                             out=bank[:, t, :],
-                            lhsT=w1_q[c, a, t][:].bitcast(E4M3X4),
-                            lhsT_scale=w1_s[c, a, t][:],
+                            lhsT=w1_q[c, a, t].bitcast(E4M3X4),
+                            lhsT_scale=w1_s[c, a, t],
                             rhs=v_w[a, h][:, jj : jj + JT].bitcast(E4M3X4),
                             rhs_scale=v_s[h][4 * a :, jj : jj + JT],
                             start=(a == 0),
@@ -226,13 +229,11 @@ def tile_list_pig_defect_scores_kernel(
                 nc.scalar.activation(
                     out=a_sq[:, JT * u : JT * (u + 1), :], in_=bank[:].rearrange("p t n -> p n t"), func=ACT.Square
                 )
-            total = ring.tile([P, JG, 4], F32, name="total")
-            nc.vector.tensor_tensor(out=total[:], in0=a_sq[:], in1=b_sq[c, g][:], op=ALU.add)
-            root = ring.tile([P, JG, 4], F32, name="root")
-            nc.scalar.activation(out=root[:], in_=total[:], func=ACT.Sqrt, bias=1.0)
-            h_bf = ring.tile([P, JG, 4], BF16, name="h_bf", align_bytes=64)
+            nc.vector.tensor_tensor(out=a_sq[:], in0=a_sq[:], in1=b_sq[c, g][:], op=ALU.add)
+            nc.scalar.activation(out=a_sq[:], in_=a_sq[:], func=ACT.Sqrt, bias=1.0)
+            h_bf = rounded_tile("h_bf", JG)
             nc.vector.tensor_tensor(
-                out=h_bf[:], in0=root[:], in1=gain_ps[:, c, 0:4].unsqueeze(1).broadcast_to([P, JG, 4]), op=ALU.mult
+                out=h_bf[:], in0=a_sq[:], in1=gain_ps[:, c, 0:4].unsqueeze(1).broadcast_to([P, JG, 4]), op=ALU.mult
             )
             h_q[c, g] = kept("h_q%d%d" % (c, g), [P, JG], U32)
             h_s[c, g] = kept("h_s%d%d" % (c, g), [P, JG], U8)
@@ -266,15 +267,10 @@ def tile_list_pig_defect_scores_kernel(
 
         for step, (c, g) in enumerate(order):
             make_h(c, g)
-            if step == 0:
-                round_w1(1, 0)
-                quantise_w1(1, 0)
-            if step == 1:
-                round_w1(1, 1)
-                quantise_w1(1, 1)
-            if step == 2:
-                quantise_w3(0, nc.scalar.copy)
-            if step == 3:
-                quantise_w3(1, nc.vector.tensor_copy)
+            if step < 2:
+                round_w1(1, step, 0, 16, nc.vector.tensor_copy)
+                quantise_w1(1, step, 1)
+            elif step < 4:
+                quantise_w3(step - 2, nc.scalar.copy if step == 2 else nc.vector.tensor_copy)
             if c == 1:
                 make_out(g)

@@ -22,6 +22,7 @@ PASS = 512
 JT = 128
 JG = 256
 HALF = 512
+V_PLANE = (12, 0)
 
 
 def load_scales(queue, plane, rows):
@@ -47,9 +48,9 @@ def tile_list_pig_defect_scores_kernel(
         wk_s = kept("wk_s", [P, N], U8)
         gain_rows = kept("gain_rows", [P, 2 * P], F32)
         warm = kept("warm", [P, 2], F32)
-        nc.gpsimd.memset(w2_s_raw[:].bitcast(I32), 0)
+        nc.gpsimd.memset(tab_s[:].bitcast(I32), 0)
         nc.gpsimd.memset(xs_s[:].bitcast(I32), 0)
-        nc.vector.memset(tab_s[:].bitcast(I32), 0)
+        nc.vector.memset(w2_s_raw[:].bitcast(I32), 0)
         nc.vector.memset(warm[:, 0:1], 1.0)
         nc.vector.memset(gain_rows[:], 0.0)
         nc.vector.memset(wk_s[:].bitcast(I32), 0)
@@ -57,15 +58,15 @@ def tile_list_pig_defect_scores_kernel(
 
         offsets = keep.tile([P, S // 16], U16, name="offsets")
         nc.sync.dma_start(offsets[:], offs)
-        xs_w = kept("xs_w", [P, S], I32)
-        nc.sync.dma_start(out=xs_w[:], in_=xs_words[0].rearrange("p c i -> p (c i)").bitcast(I32))
+        nc.sync.dma_start(out=tab_s[12:44, :].bitcast(I32), in_=tab_scales.rearrange("a q t -> (a q) t").bitcast(I32))
         w2_w_raw = kept("w2_w_raw", [P, H // 2], I32)
         nc.sync.dma_start(out=w2_w_raw[:], in_=w2_words[0].bitcast(I32))
         load_scales(nc.sync, w2_s_raw, w2_scales[0])
-        for q in range(4):
-            nc.gpsimd.dma_start(
-                out=tab_s[32 * q : 32 * q + 8, :].bitcast(I32), in_=tab_scales[:, 4 * q : 4 * q + 4, :].bitcast(I32)
-            )
+        xs_w = kept("xs_w", [P, S], I32)
+        nc.sync.dma_start(out=xs_w[:], in_=xs_words[0].rearrange("p c i -> p (c i)").bitcast(I32))
+        nc.gpsimd.dma_start(
+            out=gain_rows[0:4, :].rearrange("t (b i) -> t b i", i=8), in_=gain.rearrange("(b t i) -> t b i", t=4, i=8)
+        )
         tab_w = [kept("tab_w%d" % a, [P, T], I32) for a in range(2)]
 
         def load_table(a):
@@ -73,31 +74,16 @@ def tile_list_pig_defect_scores_kernel(
 
         w1_raw = {}
 
-        def load_w1(c, a, lo, hi):
-            w1_raw[c, a, lo] = kept("w1_raw%d%d%d" % (c, a, lo), [P, 4, 32 * (hi - lo)], F32)
-            rows = w1[PASS * a : PASS * (a + 1), PASS * c + 32 * lo : PASS * c + 32 * hi]
-            nc.sync.dma_start(out=w1_raw[c, a, lo][:], in_=rows.rearrange("(p j) n -> p j n", j=4))
+        def load_w1(c, a):
+            w1_raw[c, a] = kept("w1_raw%d%d" % (c, a), [P, 4, PASS], F32)
+            rows = w1[PASS * a : PASS * (a + 1), PASS * c : PASS * (c + 1)]
+            nc.sync.dma_start(out=w1_raw[c, a][:], in_=rows.rearrange("(p j) n -> p j n", j=4))
 
-        load_table(0)
+        load_w1(0, 0)
         load_scales(nc.sync, xs_s, xs_scales[0])
-        load_w1(0, 0, 0, 16)
+        load_w1(0, 1)
+        load_table(0)
         load_table(1)
-        load_w1(0, 1, 0, 8)
-        load_w1(0, 1, 8, 16)
-        load_w1(1, 0, 0, 16)
-        load_w1(1, 1, 0, 16)
-        nc.gpsimd.dma_start(
-            out=gain_rows[0:4, :].rearrange("t (b i) -> t b i", i=8), in_=gain.rearrange("(b t i) -> t b i", t=4, i=8)
-        )
-        load_scales(nc.gpsimd, wk_s, wk_scales[0])
-        wk_w = kept("wk_w", [P, N], I32)
-        nc.sync.dma_start(out=wk_w[:], in_=wk_words[0].rearrange("p c i -> p (c i)").bitcast(I32))
-        w3_raw = {}
-        for c in range(2):
-            w3_raw[c] = kept("w3_raw%d" % c, [P, 4, N], F32)
-            rows = w3[PASS * c : PASS * (c + 1), :].rearrange("(g t i) n -> t g i n", t=4, i=8)
-            for t in range(4):
-                nc.sync.dma_start(out=w3_raw[c][:, t, :], in_=rows[t])
 
         w2_w = kept("w2_w", [P, H // 2], I32)
         w2_s = kept("w2_s", [P, H], U8)
@@ -109,6 +95,29 @@ def tile_list_pig_defect_scores_kernel(
             out=w2_s[:].bitcast(I32).rearrange("p (c t g e) -> p c t g e", c=2, t=4, e=2),
             in_=w2_s_raw[:].bitcast(I32).rearrange("p (c g t e) -> p c t g e", c=2, t=4, e=2),
         )
+
+        picked_s = kept("picked_s", [P, S], U8)
+        nc.vector.tensor_copy(picked_s[:], tab_s[:].indirect(offsets[:]))
+        v_s = kept("v_s", [P, S], U8)
+        nc.vector.tensor_copy(out=v_s[:].bitcast(I32), in_=picked_s[:].bitcast(I32))
+        for a in range(2):
+            for q in range(4):
+                src = 12 + 16 * a + 4 * q
+                dst = 32 * q + V_PLANE[a]
+                if src != dst:
+                    nc.sync.dma_start(out=v_s[dst : dst + 4, :].bitcast(I32), in_=picked_s[src : src + 4, :].bitcast(I32))
+
+        load_w1(1, 0)
+        load_w1(1, 1)
+        w3_raw = {}
+        for c in range(2):
+            w3_raw[c] = kept("w3_raw%d" % c, [P, 4, N], F32)
+            rows = w3[PASS * c : PASS * (c + 1), :].rearrange("(g t i) n -> t g i n", t=4, i=8)
+            for t in range(4):
+                nc.sync.dma_start(out=w3_raw[c][:, t, :], in_=rows[t])
+        wk_w = kept("wk_w", [P, N], I32)
+        nc.sync.dma_start(out=wk_w[:], in_=wk_words[0].rearrange("p c i -> p (c i)").bitcast(I32))
+        load_scales(nc.sync, wk_s, wk_scales[0])
 
         ident = kept("ident", [P, P], F32)
         make_identity(nc, ident[:])
@@ -140,29 +149,23 @@ def tile_list_pig_defect_scores_kernel(
                 )
 
         v_w = {}
-        v_s = {}
 
         def gather_words(a, h):
             v_w[a, h] = kept("v_w%d%d" % (a, h), [P, HALF], U32)
             nc.vector.tensor_copy(v_w[a, h][:], tab_w[a][:].bitcast(U32).indirect(offsets[:, 32 * h : 32 * (h + 1)]))
-
-        def gather_scales(h):
-            v_s[h] = kept("v_s%d" % h, [P, HALF], U8)
-            nc.vector.tensor_copy(v_s[h][:], tab_s[:].indirect(offsets[:, 32 * h : 32 * (h + 1)]))
 
         w1_q = {}
         w1_s = {}
         w1_bf = {}
 
         def rounded_tile(name, columns):
-            return ring.tile([P, columns, 4], BF16, name=name, tag="rounded", align_bytes=64)
+            return ring.tile([P, columns, 4], BF16, name=name, align_bytes=64)
 
-        def round_w1(c, a, lo, hi, engine_copy):
-            if lo == 0:
-                w1_bf[c, a] = rounded_tile("w1_bf", PASS)
+        def round_w1(c, a, engine_copy):
+            w1_bf[c, a] = rounded_tile("w1_bf", PASS)
             for t in range(4):
-                src = w1_raw[c, a, lo][:].rearrange("p j (g t e i) -> p t g e j i", t=4, e=2, i=4)[:, t]
-                dst = w1_bf[c, a][:, P * t + 8 * lo : P * t + 8 * hi, :].rearrange("p (g e i) j -> p g e j i", e=2, i=4)
+                src = w1_raw[c, a][:].rearrange("p j (g t e i) -> p t g e j i", t=4, e=4, i=2)[:, t]
+                dst = w1_bf[c, a][:, P * t : P * (t + 1), :].rearrange("p (g e i) j -> p g e j i", e=4, i=2)
                 engine_copy(out=dst, in_=src)
 
         def quantise_w1(c, a, pieces):
@@ -180,26 +183,24 @@ def tile_list_pig_defect_scores_kernel(
                     w1_q[c, a, t] = codes[:, m0 : m0 + P]
                     w1_s[c, a, t] = scales[:, m0 : m0 + P]
 
-        gather_scales(0)
-        gather_scales(1)
+        for a in range(2):
+            round_w1(0, a, nc.vector.tensor_copy)
+            quantise_w1(0, a, 1)
         gather_words(0, 0)
         gather_words(0, 1)
-        round_w1(0, 0, 0, 16, nc.vector.tensor_copy)
-        quantise_w1(0, 0, 1)
         gather_words(1, 0)
-        gather_words(1, 1)
-        round_w1(0, 1, 0, 8, nc.vector.tensor_copy)
-        round_w1(0, 1, 8, 16, nc.vector.tensor_copy)
-        quantise_w1(0, 1, 4)
 
         w3_q = {}
         w3_s = {}
 
-        def quantise_w3(c, engine_copy):
+        def quantise_w3(c, scalar_columns):
             w3_bf = rounded_tile("w3_bf", N)
-            engine_copy(
-                out=w3_bf[:].rearrange("p (m i) t -> p m t i", i=4), in_=w3_raw[c][:].rearrange("p t (m i) -> p m t i", i=4)
-            )
+            for engine_copy, lo, hi in ((nc.scalar.copy, 0, scalar_columns), (nc.vector.tensor_copy, scalar_columns, N)):
+                if hi > lo:
+                    engine_copy(
+                        out=w3_bf[:, lo:hi, :].rearrange("p (m i) t -> p m t i", i=2),
+                        in_=w3_raw[c][:, :, lo:hi].rearrange("p t (m i) -> p m t i", i=2),
+                    )
             w3_q[c] = kept("w3_q%d" % c, [P, N], U32)
             w3_s[c] = kept("w3_s%d" % c, [P, N], U8)
             nc.vector.quantize_mx(
@@ -209,11 +210,13 @@ def tile_list_pig_defect_scores_kernel(
         h_q = {}
         h_s = {}
 
-        def make_h(c, g):
-            a_sq = ring.tile([P, JG, 4], F32, name="a_sq", bufs=4)
-            for u in range(2):
-                j0 = JG * g + JT * u
-                h, jj = divmod(j0, HALF)
+        def work_tile(name, shape, dtype):
+            return ring.tile(shape, dtype, name=name, tag="work", bufs=3, align_bytes=64)
+
+        def make_h(c, j0, width):
+            a_sq = work_tile("a_sq", [P, width, 4], F32)
+            for u0 in range(0, width, JT):
+                h, jj = divmod(j0 + u0, HALF)
                 bank = psum.tile([P, 4, JT], F32, name="ab_bank", bufs=3)
                 for t in range(4):
                     for a in range(2):
@@ -222,33 +225,40 @@ def tile_list_pig_defect_scores_kernel(
                             lhsT=w1_q[c, a, t].bitcast(E4M3X4),
                             lhsT_scale=w1_s[c, a, t],
                             rhs=v_w[a, h][:, jj : jj + JT].bitcast(E4M3X4),
-                            rhs_scale=v_s[h][4 * a :, jj : jj + JT],
+                            rhs_scale=v_s[V_PLANE[a] :, j0 + u0 : j0 + u0 + JT],
                             start=(a == 0),
                             stop=(a == 1),
                         )
                 nc.scalar.activation(
-                    out=a_sq[:, JT * u : JT * (u + 1), :], in_=bank[:].rearrange("p t n -> p n t"), func=ACT.Square
+                    out=a_sq[:, u0 : u0 + JT, :], in_=bank[:].rearrange("p t n -> p n t"), func=ACT.Square
                 )
-            nc.vector.tensor_tensor(out=a_sq[:], in0=a_sq[:], in1=b_sq[c, g][:], op=ALU.add)
+            g, gj = divmod(j0, JG)
+            nc.vector.tensor_tensor(out=a_sq[:], in0=a_sq[:], in1=b_sq[c, g][:, gj : gj + width, :], op=ALU.add)
             nc.scalar.activation(out=a_sq[:], in_=a_sq[:], func=ACT.Sqrt, bias=1.0)
-            h_bf = rounded_tile("h_bf", JG)
+            h_bf = rounded_tile("h_bf", width)
             nc.vector.tensor_tensor(
-                out=h_bf[:], in0=a_sq[:], in1=gain_ps[:, c, 0:4].unsqueeze(1).broadcast_to([P, JG, 4]), op=ALU.mult
+                out=h_bf[:], in0=a_sq[:], in1=gain_ps[:, c, 0:4].unsqueeze(1).broadcast_to([P, width, 4]), op=ALU.mult
             )
-            h_q[c, g] = kept("h_q%d%d" % (c, g), [P, JG], U32)
-            h_s[c, g] = kept("h_s%d%d" % (c, g), [P, JG], U8)
+            if gj == 0:
+                h_q[c, g] = kept("h_q%d%d" % (c, g), [P, JG], U32)
+                h_s[c, g] = kept("h_s%d%d" % (c, g), [P, JG], U8)
             nc.vector.quantize_mx(
-                out=h_q[c, g][:].bitcast(E4M3X4), scales=h_s[c, g][:], in_=h_bf[:].rearrange("p n t -> p (n t)")
+                out=h_q[c, g][:, gj : gj + width].bitcast(E4M3X4),
+                scales=h_s[c, g][:, gj : gj + width],
+                in_=h_bf[:].rearrange("p n t -> p (n t)"),
             )
 
         out_view = out.rearrange("(m p) j -> p m j", p=P)
 
-        def make_out(g):
-            cols = slice(JG * g, JG * (g + 1))
+        def make_out(j0, width, copies):
+            cols = slice(j0, j0 + width)
+            g, gj = divmod(j0, JG)
             for pair in range(2):
-                bank = psum.tile([P, 2, JG], F32, name="out_bank", bufs=4)
+                bank = psum.tile([P, 2, width], F32, name="out_bank", bufs=4)
                 passes = [(wk_w, wk_s, xs_w[:, cols], xs_s[:, cols])]
-                passes.extend((w3_q[c], w3_s[c], h_q[c, g][:], h_s[c, g][:]) for c in range(2))
+                passes.extend(
+                    (w3_q[c], w3_s[c], h_q[c, g][:, gj : gj + width], h_s[c, g][:, gj : gj + width]) for c in range(2)
+                )
                 for step, (w_codes, w_scales, x_codes, x_scales) in enumerate(passes):
                     for m in range(2):
                         n0 = P * (2 * pair + m)
@@ -261,16 +271,24 @@ def tile_list_pig_defect_scores_kernel(
                             start=(step == 0 and m == 0),
                             stop=(step == 2 and m == 1),
                         )
-                staged = ring.tile([P, 2, JG], F32, name="staged", bufs=4)
-                nc.scalar.copy(out=staged[:], in_=bank[:])
+                staged = ring.tile([P, 2, width], F32, name="staged", bufs=4)
+                copies[pair](out=staged[:], in_=bank[:])
                 nc.sync.dma_start(out=out_view[:, 2 * pair : 2 * pair + 2, cols], in_=staged[:])
 
-        for step, (c, g) in enumerate(order):
-            make_h(c, g)
-            if step < 2:
-                round_w1(1, step, 0, 16, nc.vector.tensor_copy)
-                quantise_w1(1, step, 1)
-            elif step < 4:
-                quantise_w3(step - 2, nc.scalar.copy if step == 2 else nc.vector.tensor_copy)
-            if c == 1:
-                make_out(g)
+        make_h(0, 0, JT)
+        gather_words(1, 1)
+        make_h(0, JT, JT)
+        for g in range(1, 4):
+            if g < 3:
+                round_w1(1, g - 1, nc.vector.tensor_copy)
+                quantise_w1(1, g - 1, 1)
+            else:
+                quantise_w3(0, N)
+            make_h(0, JG * g, JG)
+        quantise_w3(1, N // 2)
+        for g in range(3):
+            make_h(1, JG * g, JG)
+            make_out(JG * g, JG, [nc.scalar.copy] * 2)
+        for j0 in range(3 * JG, S, JT):
+            make_h(1, j0, JT)
+            make_out(j0, JT, [nc.scalar.copy, nc.vector.tensor_copy])

@@ -121,32 +121,30 @@ def tile_list_pig_defect_scores_kernel(
 
         ident = kept("ident", [P, P], F32)
         make_identity(nc, ident[:])
-        gain_ps = psum.tile([P, 2, P], F32, name="gain_ps")
+        gain_ps = psum.tile([P, 2, P], F32, name="out_bank", bufs=4)
         for c in range(2):
             nc.tensor.transpose(gain_ps[:, c, :], gain_rows[:, P * c : P * (c + 1)], ident[:])
-
-        order = [(c, g) for c in range(2) for g in range(4)]
+        gain_sb = kept("gain_sb", [P, 2, 4], F32)
+        nc.vector.tensor_copy(out=gain_sb[:], in_=gain_ps[:, :, 0:4])
 
         b_sq = {}
-        for c, g in order:
-            b_sq[c, g] = kept("b_sq%d%d" % (c, g), [P, JG, 4], F32)
-            for u in range(2):
-                j0 = JG * g + JT * u
-                bank = psum.tile([P, 4, JT], F32, name="ab_bank", bufs=3)
+        for c in range(2):
+            for h in range(2):
+                b_sq[c, h] = kept("b_sq%d%d" % (c, h), [P, 4, HALF], F32)
+                cols = slice(HALF * h, HALF * (h + 1))
                 for t in range(4):
                     r0 = PASS * c + P * t
+                    bank = psum.tile([P, HALF], F32, name="ab_bank", bufs=4)
                     nc.tensor.matmul_mx(
-                        out=bank[:, t, :],
+                        out=bank[:],
                         lhsT=w2_w[:, r0 // 2 : (r0 + P) // 2].bitcast(E2M1X4),
                         lhsT_scale=w2_s[:, r0 : r0 + P],
-                        rhs=xs_w[:, j0 : j0 + JT].bitcast(E4M3X4),
-                        rhs_scale=xs_s[:, j0 : j0 + JT],
+                        rhs=xs_w[:, cols].bitcast(E4M3X4),
+                        rhs_scale=xs_s[:, cols],
                         start=True,
                         stop=True,
                     )
-                nc.scalar.activation(
-                    out=b_sq[c, g][:, JT * u : JT * (u + 1), :], in_=bank[:].rearrange("p t n -> p n t"), func=ACT.Square
-                )
+                    nc.scalar.activation(out=b_sq[c, h][:, t, :], in_=bank[:], func=ACT.Square)
 
         v_w = {}
 
@@ -163,10 +161,10 @@ def tile_list_pig_defect_scores_kernel(
 
         def round_w1(c, a, engine_copy):
             w1_bf[c, a] = rounded_tile("w1_bf", PASS)
-            for t in range(4):
-                src = w1_raw[c, a][:].rearrange("p j (g t e i) -> p t g e j i", t=4, e=4, i=2)[:, t]
-                dst = w1_bf[c, a][:, P * t : P * (t + 1), :].rearrange("p (g e i) j -> p g e j i", e=4, i=2)
-                engine_copy(out=dst, in_=src)
+            engine_copy(
+                out=w1_bf[c, a][:].rearrange("p (t g i) j -> p t g i j", t=4, i=8),
+                in_=w1_raw[c, a][:].rearrange("p j (g t i) -> p t g i j", t=4, i=8),
+            )
 
         def quantise_w1(c, a, pieces):
             width = PASS // pieces
@@ -197,10 +195,7 @@ def tile_list_pig_defect_scores_kernel(
             w3_bf = rounded_tile("w3_bf", N)
             for engine_copy, lo, hi in ((nc.scalar.copy, 0, scalar_columns), (nc.vector.tensor_copy, scalar_columns, N)):
                 if hi > lo:
-                    engine_copy(
-                        out=w3_bf[:, lo:hi, :].rearrange("p (m i) t -> p m t i", i=2),
-                        in_=w3_raw[c][:, :, lo:hi].rearrange("p t (m i) -> p m t i", i=2),
-                    )
+                    engine_copy(out=w3_bf[:, lo:hi, :], in_=w3_raw[c][:, :, lo:hi].rearrange("p t m -> p m t"))
             w3_q[c] = kept("w3_q%d" % c, [P, N], U32)
             w3_s[c] = kept("w3_s%d" % c, [P, N], U8)
             nc.vector.quantize_mx(
@@ -214,30 +209,35 @@ def tile_list_pig_defect_scores_kernel(
             return ring.tile(shape, dtype, name=name, tag="work", bufs=3, align_bytes=64)
 
         def make_h(c, j0, width):
-            a_sq = work_tile("a_sq", [P, width, 4], F32)
-            for u0 in range(0, width, JT):
-                h, jj = divmod(j0 + u0, HALF)
-                bank = psum.tile([P, 4, JT], F32, name="ab_bank", bufs=3)
-                for t in range(4):
+            a_sq = work_tile("a_sq", [P, 4, width], F32)
+            h, jj = divmod(j0, HALF)
+            per_bank = HALF // width
+            for t0 in range(0, 4, per_bank):
+                bank = psum.tile([P, per_bank, width], F32, name="ab_bank", bufs=4)
+                for u in range(per_bank):
                     for a in range(2):
                         nc.tensor.matmul_mx(
-                            out=bank[:, t, :],
-                            lhsT=w1_q[c, a, t].bitcast(E4M3X4),
-                            lhsT_scale=w1_s[c, a, t],
-                            rhs=v_w[a, h][:, jj : jj + JT].bitcast(E4M3X4),
-                            rhs_scale=v_s[V_PLANE[a] :, j0 + u0 : j0 + u0 + JT],
+                            out=bank[:, u, :],
+                            lhsT=w1_q[c, a, t0 + u].bitcast(E4M3X4),
+                            lhsT_scale=w1_s[c, a, t0 + u],
+                            rhs=v_w[a, h][:, jj : jj + width].bitcast(E4M3X4),
+                            rhs_scale=v_s[V_PLANE[a] :, j0 : j0 + width],
                             start=(a == 0),
                             stop=(a == 1),
                         )
-                nc.scalar.activation(
-                    out=a_sq[:, u0 : u0 + JT, :], in_=bank[:].rearrange("p t n -> p n t"), func=ACT.Square
-                )
+                nc.scalar.activation(out=a_sq[:, t0 : t0 + per_bank, :], in_=bank[:], func=ACT.Square)
             g, gj = divmod(j0, JG)
-            nc.vector.tensor_tensor(out=a_sq[:], in0=a_sq[:], in1=b_sq[c, g][:, gj : gj + width, :], op=ALU.add)
-            nc.scalar.activation(out=a_sq[:], in_=a_sq[:], func=ACT.Sqrt, bias=1.0)
+            nc.vector.tensor_tensor(out=a_sq[:], in0=a_sq[:], in1=b_sq[c, h][:, :, jj : jj + width], op=ALU.add)
+            root = ring.tile([P, width, 4], F32, name="root")
+            nc.scalar.activation(
+                out=root[:].rearrange("p (n i) t -> p n t i", i=2),
+                in_=a_sq[:].rearrange("p t (n i) -> p n t i", i=2),
+                func=ACT.Sqrt,
+                bias=1.0,
+            )
             h_bf = rounded_tile("h_bf", width)
             nc.vector.tensor_tensor(
-                out=h_bf[:], in0=a_sq[:], in1=gain_ps[:, c, 0:4].unsqueeze(1).broadcast_to([P, width, 4]), op=ALU.mult
+                out=h_bf[:], in0=root[:], in1=gain_sb[:, c, :].unsqueeze(1).broadcast_to([P, width, 4]), op=ALU.mult
             )
             if gj == 0:
                 h_q[c, g] = kept("h_q%d%d" % (c, g), [P, JG], U32)
@@ -280,15 +280,15 @@ def tile_list_pig_defect_scores_kernel(
         make_h(0, JT, JT)
         for g in range(1, 4):
             if g < 3:
-                round_w1(1, g - 1, nc.vector.tensor_copy)
+                round_w1(1, g - 1, nc.vector.tensor_copy if g == 1 else nc.scalar.copy)
                 quantise_w1(1, g - 1, 1)
             else:
                 quantise_w3(0, N)
             make_h(0, JG * g, JG)
-        quantise_w3(1, N // 2)
+        quantise_w3(1, 0)
         for g in range(3):
             make_h(1, JG * g, JG)
-            make_out(JG * g, JG, [nc.scalar.copy] * 2)
+            make_out(JG * g, JG, [nc.scalar.copy, nc.scalar.copy if g == 0 else nc.vector.tensor_copy])
         for j0 in range(3 * JG, S, JT):
             make_h(1, j0, JT)
             make_out(j0, JT, [nc.scalar.copy, nc.vector.tensor_copy])

@@ -19,15 +19,18 @@ ALU = mybir.AluOpType
 
 P = 128
 PASS = 512
-JT = 128
-JG = 256
+BANK = 512
 HALF = 512
+STEP = 256
+SHORT = 128
+
+TAB_ROW0 = 12
 V_PLANE = (12, 0)
 
 
-def load_scales(queue, plane, rows):
+def load_plane(nc, plane, rows):
     for q in range(4):
-        queue.dma_start(out=plane[32 * q : 32 * q + 4, :].bitcast(I32), in_=rows[4 * q : 4 * q + 4, :].bitcast(I32))
+        nc.sync.dma_start(out=plane[32 * q : 32 * q + 4, :].bitcast(I32), in_=rows[4 * q : 4 * q + 4, :].bitcast(I32))
 
 
 def tile_list_pig_defect_scores_kernel(
@@ -37,10 +40,19 @@ def tile_list_pig_defect_scores_kernel(
     with ExitStack() as ctx:
         keep = ctx.enter_context(tc.tile_pool(name="keep", bufs=1))
         ring = ctx.enter_context(tc.tile_pool(name="ring", bufs=2))
-        psum = ctx.enter_context(tc.psum_pool(name="psum", bufs=1))
+        psum = ctx.enter_context(tc.psum_pool(name="psum", bufs=4))
 
         def kept(name, shape, dtype):
             return keep.tile(shape, dtype, name=name, align_bytes=64)
+
+        def product_bank(shape):
+            return psum.tile(shape, F32, name="product_bank")
+
+        def sum_bank(shape):
+            return psum.tile(shape, F32, name="sum_bank")
+
+        def rounded_tile(name, columns):
+            return ring.tile([P, columns, 4], BF16, name=name, bufs=3, align_bytes=64)
 
         xs_s = kept("xs_s", [P, S], U8)
         w2_s_raw = kept("w2_s_raw", [P, H], U8)
@@ -58,16 +70,19 @@ def tile_list_pig_defect_scores_kernel(
 
         offsets = keep.tile([P, S // 16], U16, name="offsets")
         nc.sync.dma_start(offsets[:], offs)
-        nc.sync.dma_start(out=tab_s[12:44, :].bitcast(I32), in_=tab_scales.rearrange("a q t -> (a q) t").bitcast(I32))
+        nc.sync.dma_start(
+            out=tab_s[TAB_ROW0 : TAB_ROW0 + 32, :].bitcast(I32),
+            in_=tab_scales.rearrange("a q t -> (a q) t").bitcast(I32),
+        )
         w2_w_raw = kept("w2_w_raw", [P, H // 2], I32)
         nc.sync.dma_start(out=w2_w_raw[:], in_=w2_words[0].bitcast(I32))
-        load_scales(nc.sync, w2_s_raw, w2_scales[0])
+        load_plane(nc, w2_s_raw, w2_scales[0])
         xs_w = kept("xs_w", [P, S], I32)
         nc.sync.dma_start(out=xs_w[:], in_=xs_words[0].rearrange("p c i -> p (c i)").bitcast(I32))
         nc.gpsimd.dma_start(
             out=gain_rows[0:4, :].rearrange("t (b i) -> t b i", i=8), in_=gain.rearrange("(b t i) -> t b i", t=4, i=8)
         )
-        tab_w = [kept("tab_w%d" % a, [P, T], I32) for a in range(2)]
+        tab_w = [keep.tile([P, T], I32, name="tab_w%d" % a, tag="table%d" % a, align_bytes=64) for a in range(2)]
 
         def load_table(a):
             nc.sync.dma_start(out=tab_w[a][:], in_=tab_words[a].rearrange("p t i -> p (t i)").bitcast(I32))
@@ -80,10 +95,9 @@ def tile_list_pig_defect_scores_kernel(
             nc.sync.dma_start(out=w1_raw[c, a][:], in_=rows.rearrange("(p j) n -> p j n", j=4))
 
         load_w1(0, 0)
-        load_scales(nc.sync, xs_s, xs_scales[0])
+        load_plane(nc, xs_s, xs_scales[0])
         load_w1(0, 1)
         load_table(0)
-        load_table(1)
 
         w2_w = kept("w2_w", [P, H // 2], I32)
         w2_s = kept("w2_s", [P, H], U8)
@@ -102,11 +116,12 @@ def tile_list_pig_defect_scores_kernel(
         nc.vector.tensor_copy(out=v_s[:].bitcast(I32), in_=picked_s[:].bitcast(I32))
         for a in range(2):
             for q in range(4):
-                src = 12 + 16 * a + 4 * q
+                src = TAB_ROW0 + 16 * a + 4 * q
                 dst = 32 * q + V_PLANE[a]
                 if src != dst:
                     nc.sync.dma_start(out=v_s[dst : dst + 4, :].bitcast(I32), in_=picked_s[src : src + 4, :].bitcast(I32))
 
+        load_table(1)
         load_w1(1, 0)
         load_w1(1, 1)
         w3_raw = {}
@@ -117,73 +132,72 @@ def tile_list_pig_defect_scores_kernel(
                 nc.sync.dma_start(out=w3_raw[c][:, t, :], in_=rows[t])
         wk_w = kept("wk_w", [P, N], I32)
         nc.sync.dma_start(out=wk_w[:], in_=wk_words[0].rearrange("p c i -> p (c i)").bitcast(I32))
-        load_scales(nc.sync, wk_s, wk_scales[0])
+        load_plane(nc, wk_s, wk_scales[0])
 
         ident = kept("ident", [P, P], F32)
         make_identity(nc, ident[:])
-        gain_ps = psum.tile([P, 2, P], F32, name="out_bank", bufs=4)
+        gain_ps = sum_bank([P, 2, P])
         for c in range(2):
             nc.tensor.transpose(gain_ps[:, c, :], gain_rows[:, P * c : P * (c + 1)], ident[:])
         gain_sb = kept("gain_sb", [P, 2, 4], F32)
         nc.vector.tensor_copy(out=gain_sb[:], in_=gain_ps[:, :, 0:4])
 
-        b_sq = {}
-        for c in range(2):
-            for h in range(2):
-                b_sq[c, h] = kept("b_sq%d%d" % (c, h), [P, 4, HALF], F32)
-                cols = slice(HALF * h, HALF * (h + 1))
-                for t in range(4):
-                    r0 = PASS * c + P * t
-                    bank = psum.tile([P, HALF], F32, name="ab_bank", bufs=4)
-                    nc.tensor.matmul_mx(
-                        out=bank[:],
-                        lhsT=w2_w[:, r0 // 2 : (r0 + P) // 2].bitcast(E2M1X4),
-                        lhsT_scale=w2_s[:, r0 : r0 + P],
-                        rhs=xs_w[:, cols].bitcast(E4M3X4),
-                        rhs_scale=xs_s[:, cols],
-                        start=True,
-                        stop=True,
-                    )
-                    nc.scalar.activation(out=b_sq[c, h][:, t, :], in_=bank[:], func=ACT.Square)
+        b_sq_turned = {}
+        for j0 in range(0, S, SHORT):
+            bank = product_bank([P, PASS])
+            nc.tensor.matmul_mx(
+                out=bank[:],
+                lhsT=xs_w[:, j0 : j0 + SHORT].bitcast(E4M3X4),
+                lhsT_scale=xs_s[:, j0 : j0 + SHORT],
+                rhs=w2_w[:, 0 : PASS // 2].bitcast(E2M1X4),
+                rhs_scale=w2_s[:, 0:PASS],
+                start=True,
+                stop=True,
+            )
+            b_sq_turned[j0] = kept("b_sq_turned%d" % j0, [P, PASS], F32)
+            nc.scalar.activation(out=b_sq_turned[j0][:], in_=bank[:], func=ACT.Square)
+        b_sq_upright = {}
+        for half in range(2):
+            b_sq_upright[half] = kept("b_sq_upright%d" % half, [P, 4, HALF], F32)
+            cols = slice(HALF * half, HALF * (half + 1))
+            for t in range(4):
+                r0 = PASS + P * t
+                bank = product_bank([P, HALF])
+                nc.tensor.matmul_mx(
+                    out=bank[:],
+                    lhsT=w2_w[:, r0 // 2 : (r0 + P) // 2].bitcast(E2M1X4),
+                    lhsT_scale=w2_s[:, r0 : r0 + P],
+                    rhs=xs_w[:, cols].bitcast(E4M3X4),
+                    rhs_scale=xs_s[:, cols],
+                    start=True,
+                    stop=True,
+                )
+                nc.scalar.activation(out=b_sq_upright[half][:, t, :], in_=bank[:], func=ACT.Square)
 
         v_w = {}
 
-        def gather_words(a, h):
-            v_w[a, h] = kept("v_w%d%d" % (a, h), [P, HALF], U32)
-            nc.vector.tensor_copy(v_w[a, h][:], tab_w[a][:].bitcast(U32).indirect(offsets[:, 32 * h : 32 * (h + 1)]))
+        def gather_words(a, half):
+            v_w[a, half] = kept("v_w%d%d" % (a, half), [P, HALF], U32)
+            entries = offsets[:, HALF // 16 * half : HALF // 16 * (half + 1)]
+            nc.vector.tensor_copy(v_w[a, half][:], tab_w[a][:].bitcast(U32).indirect(entries))
 
         w1_q = {}
         w1_s = {}
-        w1_bf = {}
 
-        def rounded_tile(name, columns):
-            return ring.tile([P, columns, 4], BF16, name=name, align_bytes=64)
-
-        def round_w1(c, a, engine_copy):
-            w1_bf[c, a] = rounded_tile("w1_bf", PASS)
-            engine_copy(
-                out=w1_bf[c, a][:].rearrange("p (t g i) j -> p t g i j", t=4, i=8),
+        def quantise_w1(c, a):
+            w1_bf = rounded_tile("weight_bf", PASS)
+            nc.vector.tensor_copy(
+                out=w1_bf[:].rearrange("p (t g i) j -> p t g i j", t=4, i=8),
                 in_=w1_raw[c, a][:].rearrange("p j (g t i) -> p t g i j", t=4, i=8),
             )
-
-        def quantise_w1(c, a, pieces):
-            width = PASS // pieces
-            for piece in range(pieces):
-                codes = kept("w1_q%d%d%d" % (c, a, piece), [P, width], U32)
-                scales = kept("w1_s%d%d%d" % (c, a, piece), [P, width], U8)
-                nc.vector.quantize_mx(
-                    out=codes[:].bitcast(E4M3X4),
-                    scales=scales[:],
-                    in_=w1_bf[c, a][:, width * piece : width * (piece + 1), :].rearrange("p m j -> p (m j)"),
-                )
-                for m0 in range(0, width, P):
-                    t = (width * piece + m0) // P
-                    w1_q[c, a, t] = codes[:, m0 : m0 + P]
-                    w1_s[c, a, t] = scales[:, m0 : m0 + P]
+            w1_q[c, a] = kept("w1_q%d%d" % (c, a), [P, PASS], U32)
+            w1_s[c, a] = kept("w1_s%d%d" % (c, a), [P, PASS], U8)
+            nc.vector.quantize_mx(
+                out=w1_q[c, a][:].bitcast(E4M3X4), scales=w1_s[c, a][:], in_=w1_bf[:].rearrange("p m j -> p (m j)")
+            )
 
         for a in range(2):
-            round_w1(0, a, nc.vector.tensor_copy)
-            quantise_w1(0, a, 1)
+            quantise_w1(0, a)
         gather_words(0, 0)
         gather_words(0, 1)
         gather_words(1, 0)
@@ -191,75 +205,113 @@ def tile_list_pig_defect_scores_kernel(
         w3_q = {}
         w3_s = {}
 
-        def quantise_w3(c, scalar_columns):
-            w3_bf = rounded_tile("w3_bf", N)
-            for engine_copy, lo, hi in ((nc.scalar.copy, 0, scalar_columns), (nc.vector.tensor_copy, scalar_columns, N)):
-                if hi > lo:
-                    engine_copy(out=w3_bf[:, lo:hi, :], in_=w3_raw[c][:, :, lo:hi].rearrange("p t m -> p m t"))
+        def quantise_w3(c, rounding_copy):
+            w3_bf = rounded_tile("weight_bf", N)
+            rounding_copy(out=w3_bf[:], in_=w3_raw[c][:].rearrange("p t n -> p n t"))
             w3_q[c] = kept("w3_q%d" % c, [P, N], U32)
             w3_s[c] = kept("w3_s%d" % c, [P, N], U8)
             nc.vector.quantize_mx(
-                out=w3_q[c][:].bitcast(E4M3X4), scales=w3_s[c][:], in_=w3_bf[:].rearrange("p m t -> p (m t)")
+                out=w3_q[c][:].bitcast(E4M3X4), scales=w3_s[c][:], in_=w3_bf[:].rearrange("p n t -> p (n t)")
             )
 
-        h_q = {}
-        h_s = {}
+        def root_of(root, total):
+            nc.scalar.activation(
+                out=root.rearrange("p (n e) t -> p n t e", e=2),
+                in_=total.rearrange("p t (n e) -> p n t e", e=2),
+                func=ACT.Sqrt,
+                bias=1.0,
+            )
 
-        def work_tile(name, shape, dtype):
-            return ring.tile(shape, dtype, name=name, tag="work", bufs=3, align_bytes=64)
+        def root_turned(j0, width):
+            root = ring.tile([P, width, 4], F32, name="root", bufs=3)
+            for u0 in range(j0, j0 + width, SHORT):
+                half, jj = divmod(u0, HALF)
+                bank = product_bank([P, PASS])
+                for a in range(2):
+                    nc.tensor.matmul_mx(
+                        out=bank[:],
+                        lhsT=v_w[a, half][:, jj : jj + SHORT].bitcast(E4M3X4),
+                        lhsT_scale=v_s[V_PLANE[a] :, u0 : u0 + SHORT],
+                        rhs=w1_q[0, a][:].bitcast(E4M3X4),
+                        rhs_scale=w1_s[0, a][:],
+                        start=(a == 0),
+                        stop=(a == 1),
+                    )
+                a_sq = ring.tile([P, PASS], F32, name="a_sq_turned", bufs=4)
+                nc.scalar.activation(out=a_sq[:], in_=bank[:], func=ACT.Square)
+                total = sum_bank([P, 4, SHORT])
+                for t in range(4):
+                    for term, squares in enumerate((b_sq_turned[u0], a_sq)):
+                        nc.tensor.matmul(
+                            out=total[:, t, :],
+                            lhsT=squares[:, P * t : P * (t + 1)],
+                            rhs=ident[:],
+                            is_transpose=True,
+                            start=(term == 0),
+                            stop=(term == 1),
+                        )
+                root_of(root[:, u0 - j0 : u0 - j0 + SHORT, :], total[:])
+            return root
 
-        def make_h(c, j0, width):
-            a_sq = work_tile("a_sq", [P, 4, width], F32)
-            h, jj = divmod(j0, HALF)
-            per_bank = HALF // width
-            for t0 in range(0, 4, per_bank):
-                bank = psum.tile([P, per_bank, width], F32, name="ab_bank", bufs=4)
-                for u in range(per_bank):
+        def root_upright(j0, width):
+            total = ring.tile([P, 4, width], F32, name="total_upright", bufs=3, align_bytes=64)
+            half, jj = divmod(j0, HALF)
+            slots_per_bank = BANK // width
+            for t0 in range(0, 4, slots_per_bank):
+                bank = product_bank([P, slots_per_bank, width])
+                for u in range(slots_per_bank):
+                    w_cols = slice(P * (t0 + u), P * (t0 + u + 1))
                     for a in range(2):
                         nc.tensor.matmul_mx(
                             out=bank[:, u, :],
-                            lhsT=w1_q[c, a, t0 + u].bitcast(E4M3X4),
-                            lhsT_scale=w1_s[c, a, t0 + u],
-                            rhs=v_w[a, h][:, jj : jj + width].bitcast(E4M3X4),
+                            lhsT=w1_q[1, a][:, w_cols].bitcast(E4M3X4),
+                            lhsT_scale=w1_s[1, a][:, w_cols],
+                            rhs=v_w[a, half][:, jj : jj + width].bitcast(E4M3X4),
                             rhs_scale=v_s[V_PLANE[a] :, j0 : j0 + width],
                             start=(a == 0),
                             stop=(a == 1),
                         )
-                nc.scalar.activation(out=a_sq[:, t0 : t0 + per_bank, :], in_=bank[:], func=ACT.Square)
-            g, gj = divmod(j0, JG)
-            nc.vector.tensor_tensor(out=a_sq[:], in0=a_sq[:], in1=b_sq[c, h][:, :, jj : jj + width], op=ALU.add)
-            root = ring.tile([P, width, 4], F32, name="root")
-            nc.scalar.activation(
-                out=root[:].rearrange("p (n i) t -> p n t i", i=2),
-                in_=a_sq[:].rearrange("p t (n i) -> p n t i", i=2),
-                func=ACT.Sqrt,
-                bias=1.0,
+                nc.scalar.activation(out=total[:, t0 : t0 + slots_per_bank, :], in_=bank[:], func=ACT.Square)
+            nc.vector.tensor_tensor(
+                out=total[:], in0=total[:], in1=b_sq_upright[half][:, :, jj : jj + width], op=ALU.add
             )
+            root = ring.tile([P, width, 4], F32, name="root", bufs=3)
+            root_of(root[:], total[:])
+            return root
+
+        h_q = {}
+        h_s = {}
+
+        def make_h(c, j0, width):
+            root = root_upright(j0, width) if c == 1 else root_turned(j0, width)
             h_bf = rounded_tile("h_bf", width)
             nc.vector.tensor_tensor(
                 out=h_bf[:], in0=root[:], in1=gain_sb[:, c, :].unsqueeze(1).broadcast_to([P, width, 4]), op=ALU.mult
             )
-            if gj == 0:
-                h_q[c, g] = kept("h_q%d%d" % (c, g), [P, JG], U32)
-                h_s[c, g] = kept("h_s%d%d" % (c, g), [P, JG], U8)
+            group, jj = divmod(j0, STEP)
+            if jj == 0:
+                h_q[c, group] = kept("h_q%d%d" % (c, group), [P, STEP], U32)
+                h_s[c, group] = kept("h_s%d%d" % (c, group), [P, STEP], U8)
             nc.vector.quantize_mx(
-                out=h_q[c, g][:, gj : gj + width].bitcast(E4M3X4),
-                scales=h_s[c, g][:, gj : gj + width],
+                out=h_q[c, group][:, jj : jj + width].bitcast(E4M3X4),
+                scales=h_s[c, group][:, jj : jj + width],
                 in_=h_bf[:].rearrange("p n t -> p (n t)"),
             )
 
+        staging = keep.tile([P, 4 * S], F32, name="staging", tag="table0", align_bytes=64)
         out_view = out.rearrange("(m p) j -> p m j", p=P)
 
         def make_out(j0, width, copies):
             cols = slice(j0, j0 + width)
-            g, gj = divmod(j0, JG)
+            group, jj = divmod(j0, STEP)
+            passes = [(wk_w, wk_s, xs_w[:, cols], xs_s[:, cols])]
+            passes.extend(
+                (w3_q[c], w3_s[c], h_q[c, group][:, jj : jj + width], h_s[c, group][:, jj : jj + width])
+                for c in range(2)
+            )
             for pair in range(2):
-                bank = psum.tile([P, 2, width], F32, name="out_bank", bufs=4)
-                passes = [(wk_w, wk_s, xs_w[:, cols], xs_s[:, cols])]
-                passes.extend(
-                    (w3_q[c], w3_s[c], h_q[c, g][:, gj : gj + width], h_s[c, g][:, gj : gj + width]) for c in range(2)
-                )
-                for step, (w_codes, w_scales, x_codes, x_scales) in enumerate(passes):
+                bank = sum_bank([P, 2, width])
+                for number, (w_codes, w_scales, x_codes, x_scales) in enumerate(passes):
                     for m in range(2):
                         n0 = P * (2 * pair + m)
                         nc.tensor.matmul_mx(
@@ -268,27 +320,28 @@ def tile_list_pig_defect_scores_kernel(
                             lhsT_scale=w_scales[:, n0 : n0 + P],
                             rhs=x_codes.bitcast(E4M3X4),
                             rhs_scale=x_scales,
-                            start=(step == 0 and m == 0),
-                            stop=(step == 2 and m == 1),
+                            start=(number == 0 and m == 0),
+                            stop=(number == len(passes) - 1 and m == 1),
                         )
-                staged = ring.tile([P, 2, width], F32, name="staged", bufs=4)
-                copies[pair](out=staged[:], in_=bank[:])
-                nc.sync.dma_start(out=out_view[:, 2 * pair : 2 * pair + 2, cols], in_=staged[:])
+                first = 4 * j0 + 2 * width * pair
+                staged = staging[:, first : first + 2 * width].rearrange("p (m j) -> p m j", m=2)
+                copies[pair](out=staged, in_=bank[:])
+                nc.sync.dma_start(out=out_view[:, 2 * pair : 2 * pair + 2, cols], in_=staged)
 
-        make_h(0, 0, JT)
+        make_h(0, 0, SHORT)
         gather_words(1, 1)
-        make_h(0, JT, JT)
-        for g in range(1, 4):
-            if g < 3:
-                round_w1(1, g - 1, nc.vector.tensor_copy if g == 1 else nc.scalar.copy)
-                quantise_w1(1, g - 1, 1)
-            else:
-                quantise_w3(0, N)
-            make_h(0, JG * g, JG)
-        quantise_w3(1, 0)
-        for g in range(3):
-            make_h(1, JG * g, JG)
-            make_out(JG * g, JG, [nc.scalar.copy, nc.scalar.copy if g == 0 else nc.vector.tensor_copy])
-        for j0 in range(3 * JG, S, JT):
-            make_h(1, j0, JT)
-            make_out(j0, JT, [nc.scalar.copy, nc.vector.tensor_copy])
+        make_h(0, SHORT, SHORT)
+        quantise_w1(1, 0)
+        make_h(0, STEP, STEP)
+        quantise_w1(1, 1)
+        make_h(0, 2 * STEP, STEP)
+        quantise_w3(0, nc.scalar.copy)
+        make_h(0, 3 * STEP, STEP)
+        quantise_w3(1, nc.vector.tensor_copy)
+
+        for j0 in range(0, S - STEP, STEP):
+            make_h(1, j0, STEP)
+            make_out(j0, STEP, [nc.scalar.copy, nc.scalar.copy if j0 == 0 else nc.vector.tensor_copy])
+        for j0 in range(S - STEP, S, SHORT):
+            make_h(1, j0, SHORT)
+            make_out(j0, SHORT, [nc.scalar.copy, nc.vector.tensor_copy])

from contextlib import ExitStack

import concourse.mybir as mybir
from concourse.masks import make_identity

K, T, S, K2, H, N = 1024, 4096, 1024, 512, 1024, 512
FLOPS = 2 * S * (K * H + K2 * H + H * N + K2 * N)

F32 = mybir.dt.float32
BF16 = mybir.dt.bfloat16
I32 = mybir.dt.int32
U32 = mybir.dt.uint32
U16 = mybir.dt.uint16
U8 = mybir.dt.uint8
E4M3X4 = mybir.dt.float8_e4m3fn_x4
E2M1X4 = mybir.dt.float4_e2m1fn_x4
ACT = mybir.ActivationFunctionType
ALU = mybir.AluOpType

P = 128
PASS = 512
BANK = 512
HALF = 512
STEP = 256
SHORT = 128

TAB_ROW0 = 12
V_PLANE = (12, 0)


def load_plane(nc, plane, rows):
    for q in range(4):
        nc.sync.dma_start(out=plane[32 * q : 32 * q + 4, :].bitcast(I32), in_=rows[4 * q : 4 * q + 4, :].bitcast(I32))


def tile_list_pig_defect_scores_kernel(
    tc, tab_words, tab_scales, offs, xs_words, xs_scales, w1, w2_words, w2_scales, gain, w3, wk_words, wk_scales, out
):
    nc = tc.nc
    with ExitStack() as ctx:
        keep = ctx.enter_context(tc.tile_pool(name="keep", bufs=1))
        ring = ctx.enter_context(tc.tile_pool(name="ring", bufs=2))
        psum = ctx.enter_context(tc.psum_pool(name="psum", bufs=4))

        def kept(name, shape, dtype):
            return keep.tile(shape, dtype, name=name, align_bytes=64)

        def product_bank(shape):
            return psum.tile(shape, F32, name="product_bank")

        def sum_bank(shape):
            return psum.tile(shape, F32, name="sum_bank")

        def rounded_tile(name, columns):
            return ring.tile([P, columns, 4], BF16, name=name, bufs=3, align_bytes=64)

        xs_s = kept("xs_s", [P, S], U8)
        w2_s_raw = kept("w2_s_raw", [P, H], U8)
        tab_s = kept("tab_s", [P, T], U8)
        wk_s = kept("wk_s", [P, N], U8)
        gain_rows = kept("gain_rows", [P, 2 * P], F32)
        warm = kept("warm", [P, 2], F32)
        nc.gpsimd.memset(tab_s[:].bitcast(I32), 0)
        nc.gpsimd.memset(xs_s[:].bitcast(I32), 0)
        nc.vector.memset(w2_s_raw[:].bitcast(I32), 0)
        nc.vector.memset(warm[:, 0:1], 1.0)
        nc.vector.memset(gain_rows[:], 0.0)
        nc.vector.memset(wk_s[:].bitcast(I32), 0)
        nc.scalar.activation(out=warm[:, 1:2], in_=warm[:, 0:1], func=ACT.Sqrt)

        offsets = keep.tile([P, S // 16], U16, name="offsets")
        nc.sync.dma_start(offsets[:], offs)
        nc.sync.dma_start(
            out=tab_s[TAB_ROW0 : TAB_ROW0 + 32, :].bitcast(I32),
            in_=tab_scales.rearrange("a q t -> (a q) t").bitcast(I32),
        )
        w2_w_raw = kept("w2_w_raw", [P, H // 2], I32)
        nc.sync.dma_start(out=w2_w_raw[:], in_=w2_words[0].bitcast(I32))
        load_plane(nc, w2_s_raw, w2_scales[0])
        xs_w = kept("xs_w", [P, S], I32)
        nc.sync.dma_start(out=xs_w[:], in_=xs_words[0].rearrange("p c i -> p (c i)").bitcast(I32))
        nc.gpsimd.dma_start(
            out=gain_rows[0:4, :].rearrange("t (b i) -> t b i", i=8), in_=gain.rearrange("(b t i) -> t b i", t=4, i=8)
        )
        tab_w = [keep.tile([P, T], I32, name="tab_w%d" % a, tag="table%d" % a, align_bytes=64) for a in range(2)]

        def load_table(a):
            nc.sync.dma_start(out=tab_w[a][:], in_=tab_words[a].rearrange("p t i -> p (t i)").bitcast(I32))

        w1_raw = {}

        def load_w1(c, a):
            w1_raw[c, a] = kept("w1_raw%d%d" % (c, a), [P, 4, PASS], F32)
            rows = w1[PASS * a : PASS * (a + 1), PASS * c : PASS * (c + 1)]
            nc.sync.dma_start(out=w1_raw[c, a][:], in_=rows.rearrange("(p j) n -> p j n", j=4))

        load_w1(0, 0)
        load_plane(nc, xs_s, xs_scales[0])
        load_w1(0, 1)
        load_table(0)

        w2_w = kept("w2_w", [P, H // 2], I32)
        w2_s = kept("w2_s", [P, H], U8)
        nc.vector.tensor_copy(
            out=w2_w[:].rearrange("p (c t g e) -> p c t g e", c=2, t=4, e=4),
            in_=w2_w_raw[:].rearrange("p (c g t e) -> p c t g e", c=2, t=4, e=4),
        )
        nc.vector.tensor_copy(
            out=w2_s[:].bitcast(I32).rearrange("p (c t g e) -> p c t g e", c=2, t=4, e=2),
            in_=w2_s_raw[:].bitcast(I32).rearrange("p (c g t e) -> p c t g e", c=2, t=4, e=2),
        )

        picked_s = kept("picked_s", [P, S], U8)
        nc.vector.tensor_copy(picked_s[:], tab_s[:].indirect(offsets[:]))
        v_s = kept("v_s", [P, S], U8)
        nc.vector.tensor_copy(out=v_s[:].bitcast(I32), in_=picked_s[:].bitcast(I32))
        for a in range(2):
            for q in range(4):
                src = TAB_ROW0 + 16 * a + 4 * q
                dst = 32 * q + V_PLANE[a]
                if src != dst:
                    nc.sync.dma_start(out=v_s[dst : dst + 4, :].bitcast(I32), in_=picked_s[src : src + 4, :].bitcast(I32))

        load_table(1)
        load_w1(1, 0)
        load_w1(1, 1)
        w3_raw = {}
        for c in range(2):
            w3_raw[c] = kept("w3_raw%d" % c, [P, 4, N], F32)
            rows = w3[PASS * c : PASS * (c + 1), :].rearrange("(g t i) n -> t g i n", t=4, i=8)
            for t in range(4):
                nc.sync.dma_start(out=w3_raw[c][:, t, :], in_=rows[t])
        wk_w = kept("wk_w", [P, N], I32)
        nc.sync.dma_start(out=wk_w[:], in_=wk_words[0].rearrange("p c i -> p (c i)").bitcast(I32))
        load_plane(nc, wk_s, wk_scales[0])

        ident = kept("ident", [P, P], F32)
        make_identity(nc, ident[:])
        gain_ps = sum_bank([P, 2, P])
        for c in range(2):
            nc.tensor.transpose(gain_ps[:, c, :], gain_rows[:, P * c : P * (c + 1)], ident[:])
        gain_sb = kept("gain_sb", [P, 2, 4], F32)
        nc.vector.tensor_copy(out=gain_sb[:], in_=gain_ps[:, :, 0:4])

        b_sq_turned = {}
        for j0 in range(0, S, SHORT):
            bank = product_bank([P, PASS])
            nc.tensor.matmul_mx(
                out=bank[:],
                lhsT=xs_w[:, j0 : j0 + SHORT].bitcast(E4M3X4),
                lhsT_scale=xs_s[:, j0 : j0 + SHORT],
                rhs=w2_w[:, 0 : PASS // 2].bitcast(E2M1X4),
                rhs_scale=w2_s[:, 0:PASS],
                start=True,
                stop=True,
            )
            b_sq_turned[j0] = kept("b_sq_turned%d" % j0, [P, PASS], F32)
            nc.scalar.activation(out=b_sq_turned[j0][:], in_=bank[:], func=ACT.Square)
        b_sq_upright = {}
        for half in range(2):
            b_sq_upright[half] = kept("b_sq_upright%d" % half, [P, 4, HALF], F32)
            cols = slice(HALF * half, HALF * (half + 1))
            for t in range(4):
                r0 = PASS + P * t
                bank = product_bank([P, HALF])
                nc.tensor.matmul_mx(
                    out=bank[:],
                    lhsT=w2_w[:, r0 // 2 : (r0 + P) // 2].bitcast(E2M1X4),
                    lhsT_scale=w2_s[:, r0 : r0 + P],
                    rhs=xs_w[:, cols].bitcast(E4M3X4),
                    rhs_scale=xs_s[:, cols],
                    start=True,
                    stop=True,
                )
                nc.scalar.activation(out=b_sq_upright[half][:, t, :], in_=bank[:], func=ACT.Square)

        v_w = {}

        def gather_words(a, half):
            v_w[a, half] = kept("v_w%d%d" % (a, half), [P, HALF], U32)
            entries = offsets[:, HALF // 16 * half : HALF // 16 * (half + 1)]
            nc.vector.tensor_copy(v_w[a, half][:], tab_w[a][:].bitcast(U32).indirect(entries))

        w1_q = {}
        w1_s = {}

        def quantise_w1(c, a):
            w1_bf = rounded_tile("weight_bf", PASS)
            nc.vector.tensor_copy(
                out=w1_bf[:].rearrange("p (t g i) j -> p t g i j", t=4, i=8),
                in_=w1_raw[c, a][:].rearrange("p j (g t i) -> p t g i j", t=4, i=8),
            )
            w1_q[c, a] = kept("w1_q%d%d" % (c, a), [P, PASS], U32)
            w1_s[c, a] = kept("w1_s%d%d" % (c, a), [P, PASS], U8)
            nc.vector.quantize_mx(
                out=w1_q[c, a][:].bitcast(E4M3X4), scales=w1_s[c, a][:], in_=w1_bf[:].rearrange("p m j -> p (m j)")
            )

        for a in range(2):
            quantise_w1(0, a)
        gather_words(0, 0)
        gather_words(0, 1)
        gather_words(1, 0)

        w3_q = {}
        w3_s = {}

        def quantise_w3(c, rounding_copy):
            w3_bf = rounded_tile("weight_bf", N)
            rounding_copy(out=w3_bf[:], in_=w3_raw[c][:].rearrange("p t n -> p n t"))
            w3_q[c] = kept("w3_q%d" % c, [P, N], U32)
            w3_s[c] = kept("w3_s%d" % c, [P, N], U8)
            nc.vector.quantize_mx(
                out=w3_q[c][:].bitcast(E4M3X4), scales=w3_s[c][:], in_=w3_bf[:].rearrange("p n t -> p (n t)")
            )

        def root_of(root, total):
            nc.scalar.activation(
                out=root.rearrange("p (n e) t -> p n t e", e=2),
                in_=total.rearrange("p t (n e) -> p n t e", e=2),
                func=ACT.Sqrt,
                bias=1.0,
            )

        def root_turned(j0, width):
            root = ring.tile([P, width, 4], F32, name="root", bufs=3)
            for u0 in range(j0, j0 + width, SHORT):
                half, jj = divmod(u0, HALF)
                bank = product_bank([P, PASS])
                for a in range(2):
                    nc.tensor.matmul_mx(
                        out=bank[:],
                        lhsT=v_w[a, half][:, jj : jj + SHORT].bitcast(E4M3X4),
                        lhsT_scale=v_s[V_PLANE[a] :, u0 : u0 + SHORT],
                        rhs=w1_q[0, a][:].bitcast(E4M3X4),
                        rhs_scale=w1_s[0, a][:],
                        start=(a == 0),
                        stop=(a == 1),
                    )
                a_sq = ring.tile([P, PASS], F32, name="a_sq_turned", bufs=4)
                nc.scalar.activation(out=a_sq[:], in_=bank[:], func=ACT.Square)
                total = sum_bank([P, 4, SHORT])
                for t in range(4):
                    for term, squares in enumerate((b_sq_turned[u0], a_sq)):
                        nc.tensor.matmul(
                            out=total[:, t, :],
                            lhsT=squares[:, P * t : P * (t + 1)],
                            rhs=ident[:],
                            is_transpose=True,
                            start=(term == 0),
                            stop=(term == 1),
                        )
                root_of(root[:, u0 - j0 : u0 - j0 + SHORT, :], total[:])
            return root

        def root_upright(j0, width):
            total = ring.tile([P, 4, width], F32, name="total_upright", bufs=3, align_bytes=64)
            half, jj = divmod(j0, HALF)
            slots_per_bank = BANK // width
            for t0 in range(0, 4, slots_per_bank):
                bank = product_bank([P, slots_per_bank, width])
                for u in range(slots_per_bank):
                    w_cols = slice(P * (t0 + u), P * (t0 + u + 1))
                    for a in range(2):
                        nc.tensor.matmul_mx(
                            out=bank[:, u, :],
                            lhsT=w1_q[1, a][:, w_cols].bitcast(E4M3X4),
                            lhsT_scale=w1_s[1, a][:, w_cols],
                            rhs=v_w[a, half][:, jj : jj + width].bitcast(E4M3X4),
                            rhs_scale=v_s[V_PLANE[a] :, j0 : j0 + width],
                            start=(a == 0),
                            stop=(a == 1),
                        )
                nc.scalar.activation(out=total[:, t0 : t0 + slots_per_bank, :], in_=bank[:], func=ACT.Square)
            nc.vector.tensor_tensor(
                out=total[:], in0=total[:], in1=b_sq_upright[half][:, :, jj : jj + width], op=ALU.add
            )
            root = ring.tile([P, width, 4], F32, name="root", bufs=3)
            root_of(root[:], total[:])
            return root

        h_q = {}
        h_s = {}

        def make_h(c, j0, width):
            root = root_upright(j0, width) if c == 1 else root_turned(j0, width)
            h_bf = rounded_tile("h_bf", width)
            nc.vector.tensor_tensor(
                out=h_bf[:], in0=root[:], in1=gain_sb[:, c, :].unsqueeze(1).broadcast_to([P, width, 4]), op=ALU.mult
            )
            group, jj = divmod(j0, STEP)
            if jj == 0:
                h_q[c, group] = kept("h_q%d%d" % (c, group), [P, STEP], U32)
                h_s[c, group] = kept("h_s%d%d" % (c, group), [P, STEP], U8)
            nc.vector.quantize_mx(
                out=h_q[c, group][:, jj : jj + width].bitcast(E4M3X4),
                scales=h_s[c, group][:, jj : jj + width],
                in_=h_bf[:].rearrange("p n t -> p (n t)"),
            )

        staging = keep.tile([P, 4 * S], F32, name="staging", tag="table0", align_bytes=64)
        out_view = out.rearrange("(m p) j -> p m j", p=P)

        def make_out(j0, width, copies):
            cols = slice(j0, j0 + width)
            group, jj = divmod(j0, STEP)
            passes = [(wk_w, wk_s, xs_w[:, cols], xs_s[:, cols])]
            passes.extend(
                (w3_q[c], w3_s[c], h_q[c, group][:, jj : jj + width], h_s[c, group][:, jj : jj + width])
                for c in range(2)
            )
            for pair in range(2):
                bank = sum_bank([P, 2, width])
                for number, (w_codes, w_scales, x_codes, x_scales) in enumerate(passes):
                    for m in range(2):
                        n0 = P * (2 * pair + m)
                        nc.tensor.matmul_mx(
                            out=bank[:, m, :],
                            lhsT=w_codes[:, n0 : n0 + P].bitcast(E4M3X4),
                            lhsT_scale=w_scales[:, n0 : n0 + P],
                            rhs=x_codes.bitcast(E4M3X4),
                            rhs_scale=x_scales,
                            start=(number == 0 and m == 0),
                            stop=(number == len(passes) - 1 and m == 1),
                        )
                first = 4 * j0 + 2 * width * pair
                staged = staging[:, first : first + 2 * width].rearrange("p (m j) -> p m j", m=2)
                copies[pair](out=staged, in_=bank[:])
                nc.sync.dma_start(out=out_view[:, 2 * pair : 2 * pair + 2, cols], in_=staged)

        make_h(0, 0, SHORT)
        gather_words(1, 1)
        make_h(0, SHORT, SHORT)
        quantise_w1(1, 0)
        make_h(0, STEP, STEP)
        quantise_w1(1, 1)
        make_h(0, 2 * STEP, STEP)
        quantise_w3(0, nc.scalar.copy)
        make_h(0, 3 * STEP, STEP)
        quantise_w3(1, nc.vector.tensor_copy)

        for j0 in range(0, S - STEP, STEP):
            make_h(1, j0, STEP)
            make_out(j0, STEP, [nc.scalar.copy, nc.scalar.copy if j0 == 0 else nc.vector.tensor_copy])
        for j0 in range(S - STEP, S, SHORT):
            make_h(1, j0, SHORT)
            make_out(j0, SHORT, [nc.scalar.copy, nc.vector.tensor_copy])
